import numpy as np
import ml_dtypes


def mxq(x, axis, fmt="e4m3"):
    dtype, down = {"e4m3": (ml_dtypes.float8_e4m3fn, 7), "e5m2": (ml_dtypes.float8_e5m2, 14)}[fmt]
    v = np.moveaxis(np.asarray(x, np.float32).astype(ml_dtypes.bfloat16).astype(np.float64), axis, -1)
    blocks = v.reshape(v.shape[:-1] + (-1, 32))
    amax = np.abs(blocks).max(-1, keepdims=True)
    byte = np.maximum(np.where(amax > 0, np.frexp(amax)[1] - 1 + 127, 0) - down, 1)
    scale = np.exp2(byte - 127.0)
    codes = (blocks / scale).astype(np.float32).astype(dtype).astype(np.float64)
    return np.moveaxis((codes * scale).reshape(v.shape), -1, axis)


WIDE = False


def mx_kscale(k):
    if not WIDE:
        return np.ones(k)
    levels = np.array([10, -10, 5, -5, 0])
    if k % 512:
        return np.exp2(np.random.permutation(np.resize(levels, k // 32))).repeat(32)
    a = np.empty((k // 512, 16))
    for p in range(k // 512):
        a[p, :8] = np.random.permutation(np.resize(levels, 8))
        for g in range(8):
            far = levels[np.abs(levels - a[p, g]) >= 10]
            a[p, g + 8] = far[np.random.randint(len(far))]
    return np.exp2(a.ravel()).repeat(32)


def f64(x):
    return np.asarray(x).astype(np.float64)


def striped(idx):
    return np.tile(idx.reshape(-1, 16).T, (8, 1)).astype(np.uint16)


def unstriped(offs):
    return offs[:16].T.reshape(-1).astype(np.int64)


def pack_weight(w):
    k, n = w.shape
    w = f64(np.asarray(w, np.float32).astype(ml_dtypes.bfloat16)).reshape(k // 32, 32, n)
    amax = np.abs(w).max(1)
    byte = np.clip(np.where(amax > 0, np.frexp(amax)[1] - 1 + 127 - 7, 1), 1, 254)
    scaled = (w * np.exp2(127.0 - byte)[:, None, :]).reshape(k, n).astype(np.float32)
    words = np.ascontiguousarray(scaled.reshape(k // 512, 128, 4, n).transpose(0, 1, 3, 2)).astype(ml_dtypes.float8_e4m3fn).view(np.uint8)
    return words, np.ascontiguousarray(byte.astype(np.uint8).reshape(k // 512, 16, n))


def unpack_weight(words, scales):
    g, p, n, _ = words.shape
    vals = np.ascontiguousarray(words).view(ml_dtypes.float8_e4m3fn).astype(np.float64) * np.repeat(np.exp2(scales.astype(np.float64) - 127.0), 8, axis=1)[..., None]
    return vals.transpose(0, 1, 3, 2).reshape(g * 512, n)


K, T, S, V, R = 512, 2048, 512, 256, 128


def setup_inputs():
    n = np.random.standard_normal
    s = mx_kscale(K)[:, None]
    c = mx_kscale(S)
    packed_xT = pack_weight(n((K, T)) * s)
    return {
        "x_words": packed_xT[0],
        "x_scales": packed_xT[1],
        "rew": (n((K, V)) / np.sqrt(K) / s).astype(np.float32),
        "pert": (n((S, R)) / np.sqrt(S) / c[:, None]).astype(np.float32),
        "base": (0.5 * n((S, 1))).astype(np.float32),
        "isig": (np.random.uniform(0.6, 1.4, (S, 1)) * c[:, None]).astype(np.float32),
        "theta": (n((R, V))).astype(np.float32),
        "offs": striped(np.random.permutation(T)[:S]),
    }


def reference(x_words, x_scales, rew, pert, base, isig, theta, offs):
    xq = unpack_weight(x_words, x_scales)[:, unstriped(offs)]
    rewq = mxq(f64(rew), 0, "e4m3")
    y = xq.T @ rewq
    util = np.tanh(1.5 * (y + f64(base)))
    wu = f64(isig) * util
    grad = mxq(f64(pert), 0, "e4m3").T @ mxq(wu, 0, "e4m3")
    return 0.98 * f64(theta) + 0.5 * grad

@@ -1,0 +1,133 @@
+from contextlib import ExitStack
+
+import concourse.mybir as mybir
+
+K, T, S, V, R = 512, 2048, 512, 256, 128
+FLOPS = 2 * K * S * V + 2 * S * R * V
+
+F32 = mybir.dt.float32
+BF16 = mybir.dt.bfloat16
+I32 = mybir.dt.int32
+U32 = mybir.dt.uint32
+U16 = mybir.dt.uint16
+U8 = mybir.dt.uint8
+FP8X4 = mybir.dt.float8_e4m3fn_x4
+MULT = mybir.AluOpType.mult
+ADD = mybir.AluOpType.add
+TANH = mybir.ActivationFunctionType.Tanh
+
+P = 128
+PACK = 4
+HALVES = 2
+W = V // HALVES
+LINE = 4
+
+
+def rows_by_line(ap):
+    return ap.rearrange("p j (c i) -> p c j i", i=LINE)
+
+
+def words_by_line(ap):
+    return ap.rearrange("p (c i) j -> p c j i", i=LINE)
+
+
+def tile_picked_yevos_tanh_p_kernel(
+    tc, x_words, x_scales, rew, pert, base, isig, theta, offs, out
+):
+    nc = tc.nc
+    with ExitStack() as ctx:
+        sb = ctx.enter_context(tc.tile_pool(name="sb", bufs=1))
+        psum = ctx.enter_context(tc.psum_pool(name="psum", bufs=1))
+
+        offsets = sb.tile([P, S // 16], U16, name="offsets")
+        nc.sync.dma_start(offsets[:], offs)
+
+        all_scales = sb.tile([P, T], U8, name="all_scales", align_bytes=64)
+        nc.vector.memset(all_scales[:].bitcast(I32), 0)
+        scale_rows = x_scales[0].rearrange("(q r) c -> r q c", r=4)
+
+        rew_rows = rew.rearrange("(p j) v -> p j v", j=PACK)
+        rew_raw = [sb.tile([P, PACK, W], F32, name=f"rew_raw{h}") for h in range(HALVES)]
+        nc.sync.dma_start(rew_raw[0][:], rew_rows[:, :, 0:W])
+        for r in range(4):
+            nc.sync.dma_start(all_scales[r:P:32, :].bitcast(I32), scale_rows[r].bitcast(I32))
+        all_words = sb.tile([P, T], U32, name="all_words", align_bytes=64)
+        nc.sync.dma_start(all_words[:].bitcast(I32), x_words[0].rearrange("p c b -> p (c b)").bitcast(I32))
+        nc.sync.dma_start(rew_raw[1][:], rew_rows[:, :, W:V])
+        pert_raw = sb.tile([P, PACK, R], F32, name="pert_raw")
+        nc.sync.dma_start(pert_raw[:], pert.rearrange("(p j) r -> p j r", j=PACK))
+        theta_raw = sb.tile([P, V], F32, name="theta_raw")
+        nc.sync.dma_start(theta_raw[:], theta)
+
+        base_sb = sb.tile([P, PACK], F32, name="base_sb")
+        nc.gpsimd.dma_start(base_sb[:], base.rearrange("(p j) o -> p (j o)", j=PACK))
+        isig_sb = sb.tile([P, PACK], F32, name="isig_sb")
+        nc.gpsimd.dma_start(isig_sb[:], isig.rearrange("(p j) o -> p (j o)", j=PACK))
+        bias = sb.tile([P, PACK], F32, name="bias")
+        nc.gpsimd.tensor_scalar(bias[:], base_sb[:], 1.5, 0.0, MULT, ADD)
+
+        picked_scales = sb.tile([P, S], U8, name="picked_scales", align_bytes=64)
+        nc.vector.tensor_copy(picked_scales[:], all_scales[:].indirect(offsets[:]))
+        x_scale = sb.tile([P, PACK, P], U8, name="x_scale", align_bytes=64)
+        nc.vector.tensor_copy(x_scale[:], picked_scales[:].rearrange("p (m j) -> p j m", j=PACK))
+
+        rew_codes, rew_scales = [], []
+
+        def quantise_rew(h):
+            grouped = sb.tile([P, W, PACK], BF16, name=f"rew_bf{h}", align_bytes=64)
+            nc.scalar.copy(words_by_line(grouped[:]), rows_by_line(rew_raw[h][:]))
+            codes = sb.tile([P, W], U32, name=f"rew_codes{h}", align_bytes=64)
+            scales = sb.tile([P, W], U8, name=f"rew_scales{h}", align_bytes=64)
+            nc.vector.quantize_mx(codes[:].bitcast(FP8X4), scales[:], grouped[:].rearrange("p w j -> p (w j)"))
+            rew_codes.append(codes)
+            rew_scales.append(scales)
+
+        quantise_rew(0)
+        x_codes = sb.tile([P, PACK, P], U32, name="x_codes", align_bytes=64)
+        nc.vector.tensor_copy(x_codes[:].rearrange("p j m -> p m j"), all_words[:].indirect(offsets[:]))
+
+        quantise_rew(1)
+
+        util = []
+        for h in range(HALVES):
+            u = sb.tile([P, PACK, W], F32, name=f"util{h}")
+            for j in range(PACK):
+                y = psum.tile([P, W], F32, name=f"y{h}{j}", tag=f"bank{PACK * h + j}")
+                nc.tensor.matmul_mx(
+                    y[:], lhsT=x_codes[:, j, :].bitcast(FP8X4), lhsT_scale=x_scale[:, j, :],
+                    rhs=rew_codes[h][:].bitcast(FP8X4), rhs_scale=rew_scales[h][:], start=True, stop=True,
+                )
+                nc.scalar.activation(u[:, j, :], y[:], TANH, bias=bias[:, j : j + 1], scale=1.5)
+            util.append(u)
+
+        pert_bf = sb.tile([P, R, PACK], BF16, name="pert_bf", align_bytes=64)
+        nc.vector.tensor_copy(words_by_line(pert_bf[:]), rows_by_line(pert_raw[:]))
+        pert_codes = sb.tile([P, R], U32, name="pert_codes", align_bytes=64)
+        pert_scales = sb.tile([P, R], U8, name="pert_scales", align_bytes=64)
+        nc.vector.quantize_mx(pert_codes[:].bitcast(FP8X4), pert_scales[:], pert_bf[:].rearrange("p w j -> p (w j)"))
+
+        isig_wide = isig_sb[:].unsqueeze(1).unsqueeze(3).to_broadcast([P, W // LINE, PACK, LINE])
+        wu = []
+        for h in range(HALVES):
+            wu_bf = sb.tile([P, W, PACK], BF16, name=f"wu_bf{h}", align_bytes=64)
+            nc.vector.tensor_tensor(words_by_line(wu_bf[:]), rows_by_line(util[h][:]), isig_wide, MULT)
+            wu.append(wu_bf)
+
+        decayed = util[0][:, 0:HALVES, :]
+        nc.scalar.mul(decayed, theta_raw[:].rearrange("p (h w) -> p h w", h=HALVES), 0.98)
+
+        grads = []
+        for h in range(HALVES):
+            codes = sb.tile([P, W], U32, name=f"wu_codes{h}", align_bytes=64)
+            scales = sb.tile([P, W], U8, name=f"wu_scales{h}", align_bytes=64)
+            nc.vector.quantize_mx(codes[:].bitcast(FP8X4), scales[:], wu[h][:].rearrange("p w j -> p (w j)"))
+            grad = psum.tile([P, W], F32, name=f"grad{h}", tag=f"bank{h}")
+            nc.tensor.matmul_mx(
+                grad[:], lhsT=pert_codes[:].bitcast(FP8X4), lhsT_scale=pert_scales[:],
+                rhs=codes[:].bitcast(FP8X4), rhs_scale=scales[:], start=True, stop=True,
+            )
+            grads.append(grad)
+        for h in range(HALVES):
+            res = sb.tile([P, W], F32, name=f"res{h}")
+            nc.vector.scalar_tensor_tensor(res[:], grads[h][:], 0.5, decayed[:, h, :], MULT, ADD)
+            nc.sync.dma_start(out[:, h * W : (h + 1) * W], res[:])

@@ -20,7 +20,8 @@ P = 128
 PACK = 4
 HALVES = 2
 W = V // HALVES
-LINE = 4
+LINE = 2
+RUN = 2
 
 
 def rows_by_line(ap):
@@ -55,21 +56,28 @@ def tile_picked_yevos_tanh_p_kernel(
         nc.sync.dma_start(all_words[:].bitcast(I32), x_words[0].rearrange("p c b -> p (c b)").bitcast(I32))
         nc.sync.dma_start(rew_raw[1][:], rew_rows[:, :, W:V])
         pert_raw = sb.tile([P, PACK, R], F32, name="pert_raw")
-        nc.sync.dma_start(pert_raw[:], pert.rearrange("(p j) r -> p j r", j=PACK))
+        pert_rows = pert.rearrange("(g j c) r -> c g j r", j=PACK, c=RUN)
+        for c in range(RUN):
+            nc.sync.dma_start(pert_raw[c:P:RUN], pert_rows[c])
+        span = RUN * (PACK - 1) + 1
+        base_sb = sb.tile([P, span], F32, name="base_sb")
+        isig_sb = sb.tile([P, span], F32, name="isig_sb")
+        for dst, src in ((base_sb, base), (isig_sb, isig)):
+            groups = src.rearrange("(g e) o -> g (e o)", e=RUN * PACK)
+            for c in range(RUN):
+                nc.sync.dma_start(dst[c:P:RUN, :], groups[:, c : c + span])
         theta_raw = sb.tile([P, V], F32, name="theta_raw")
         nc.sync.dma_start(theta_raw[:], theta)
-
-        base_sb = sb.tile([P, PACK], F32, name="base_sb")
-        nc.gpsimd.dma_start(base_sb[:], base.rearrange("(p j) o -> p (j o)", j=PACK))
-        isig_sb = sb.tile([P, PACK], F32, name="isig_sb")
-        nc.gpsimd.dma_start(isig_sb[:], isig.rearrange("(p j) o -> p (j o)", j=PACK))
         bias = sb.tile([P, PACK], F32, name="bias")
-        nc.gpsimd.tensor_scalar(bias[:], base_sb[:], 1.5, 0.0, MULT, ADD)
+        nc.scalar.mul(bias[:], base_sb[:, 0:span:RUN], 1.5)
 
         picked_scales = sb.tile([P, S], U8, name="picked_scales", align_bytes=64)
         nc.vector.tensor_copy(picked_scales[:], all_scales[:].indirect(offsets[:]))
         x_scale = sb.tile([P, PACK, P], U8, name="x_scale", align_bytes=64)
-        nc.vector.tensor_copy(x_scale[:], picked_scales[:].rearrange("p (m j) -> p j m", j=PACK))
+        nc.vector.tensor_copy(
+            x_scale[:].rearrange("p j (g c) -> p j g c", c=RUN),
+            picked_scales[:].rearrange("p (g j c) -> p j g c", j=PACK, c=RUN),
+        )
 
         rew_codes, rew_scales = [], []
 
@@ -84,7 +92,7 @@ def tile_picked_yevos_tanh_p_kernel(
 
         quantise_rew(0)
         x_codes = sb.tile([P, PACK, P], U32, name="x_codes", align_bytes=64)
-        nc.vector.tensor_copy(x_codes[:].rearrange("p j m -> p m j"), all_words[:].indirect(offsets[:]))
+        nc.vector.tensor_copy(x_codes[:].rearrange("p j (g c) -> p g j c", c=RUN), all_words[:].indirect(offsets[:]))
 
         quantise_rew(1)
 
@@ -106,7 +114,7 @@ def tile_picked_yevos_tanh_p_kernel(
         pert_scales = sb.tile([P, R], U8, name="pert_scales", align_bytes=64)
         nc.vector.quantize_mx(pert_codes[:].bitcast(FP8X4), pert_scales[:], pert_bf[:].rearrange("p w j -> p (w j)"))
 
-        isig_wide = isig_sb[:].unsqueeze(1).unsqueeze(3).to_broadcast([P, W // LINE, PACK, LINE])
+        isig_wide = isig_sb[:, 0:span:RUN].unsqueeze(1).unsqueeze(3).to_broadcast([P, W // LINE, PACK, LINE])
         wu = []
         for h in range(HALVES):
             wu_bf = sb.tile([P, W, PACK], BF16, name=f"wu_bf{h}", align_bytes=64)

@@ -21,7 +21,7 @@ PACK = 4
 HALVES = 2
 W = V // HALVES
 LINE = 2
-RUN = 2
+HEAD = 256
 
 
 def rows_by_line(ap):
@@ -50,34 +50,26 @@ def tile_picked_yevos_tanh_p_kernel(
         rew_rows = rew.rearrange("(p j) v -> p j v", j=PACK)
         rew_raw = [sb.tile([P, PACK, W], F32, name=f"rew_raw{h}") for h in range(HALVES)]
         nc.sync.dma_start(rew_raw[0][:], rew_rows[:, :, 0:W])
+        all_words = sb.tile([P, T], U32, name="all_words", align_bytes=64)
+        word_rows = x_words[0].rearrange("p c b -> p (c b)").bitcast(I32)
+        nc.sync.dma_start(all_words[:, 0:HEAD].bitcast(I32), word_rows[:, 0:HEAD])
         for r in range(4):
             nc.sync.dma_start(all_scales[r:P:32, :].bitcast(I32), scale_rows[r].bitcast(I32))
-        all_words = sb.tile([P, T], U32, name="all_words", align_bytes=64)
-        nc.sync.dma_start(all_words[:].bitcast(I32), x_words[0].rearrange("p c b -> p (c b)").bitcast(I32))
+        nc.sync.dma_start(all_words[:, HEAD:T].bitcast(I32), word_rows[:, HEAD:T])
         nc.sync.dma_start(rew_raw[1][:], rew_rows[:, :, W:V])
         pert_raw = sb.tile([P, PACK, R], F32, name="pert_raw")
-        pert_rows = pert.rearrange("(g j c) r -> c g j r", j=PACK, c=RUN)
-        for c in range(RUN):
-            nc.sync.dma_start(pert_raw[c:P:RUN], pert_rows[c])
-        span = RUN * (PACK - 1) + 1
-        base_sb = sb.tile([P, span], F32, name="base_sb")
-        isig_sb = sb.tile([P, span], F32, name="isig_sb")
-        for dst, src in ((base_sb, base), (isig_sb, isig)):
-            groups = src.rearrange("(g e) o -> g (e o)", e=RUN * PACK)
-            for c in range(RUN):
-                nc.sync.dma_start(dst[c:P:RUN, :], groups[:, c : c + span])
+        nc.sync.dma_start(pert_raw[:], pert.rearrange("(p j) r -> p j r", j=PACK))
+        base_sb = sb.tile([P, PACK], F32, name="base_sb")
+        nc.sync.dma_start(base_sb[:], base.rearrange("(p j) o -> p (j o)", j=PACK))
+        isig_sb = sb.tile([P, PACK], F32, name="isig_sb")
+        nc.sync.dma_start(isig_sb[:], isig.rearrange("(p j) o -> p (j o)", j=PACK))
         theta_raw = sb.tile([P, V], F32, name="theta_raw")
         nc.sync.dma_start(theta_raw[:], theta)
         bias = sb.tile([P, PACK], F32, name="bias")
-        nc.scalar.mul(bias[:], base_sb[:, 0:span:RUN], 1.5)
+        nc.gpsimd.tensor_scalar(bias[:], base_sb[:], 1.5, 0.0, MULT, ADD)
 
         picked_scales = sb.tile([P, S], U8, name="picked_scales", align_bytes=64)
         nc.vector.tensor_copy(picked_scales[:], all_scales[:].indirect(offsets[:]))
-        x_scale = sb.tile([P, PACK, P], U8, name="x_scale", align_bytes=64)
-        nc.vector.tensor_copy(
-            x_scale[:].rearrange("p j (g c) -> p j g c", c=RUN),
-            picked_scales[:].rearrange("p (g j c) -> p j g c", j=PACK, c=RUN),
-        )
 
         rew_codes, rew_scales = [], []
 
@@ -91,21 +83,28 @@ def tile_picked_yevos_tanh_p_kernel(
             rew_scales.append(scales)
 
         quantise_rew(0)
+        x_scale = sb.tile([P, PACK, P], U8, name="x_scale", align_bytes=64)
+        nc.vector.tensor_copy(x_scale[:], picked_scales[:].rearrange("p (m j) -> p j m", j=PACK))
         x_codes = sb.tile([P, PACK, P], U32, name="x_codes", align_bytes=64)
-        nc.vector.tensor_copy(x_codes[:].rearrange("p j (g c) -> p g j c", c=RUN), all_words[:].indirect(offsets[:]))
+        nc.vector.tensor_copy(x_codes[:].rearrange("p j m -> p m j"), all_words[:].indirect(offsets[:]))
 
         quantise_rew(1)
 
-        util = []
+        chunks = [(0, 0, W), (1, 0, W // 2), (1, W // 2, W // 2)]
+        ys = []
         for h in range(HALVES):
-            u = sb.tile([P, PACK, W], F32, name=f"util{h}")
             for j in range(PACK):
                 y = psum.tile([P, W], F32, name=f"y{h}{j}", tag=f"bank{PACK * h + j}")
                 nc.tensor.matmul_mx(
                     y[:], lhsT=x_codes[:, j, :].bitcast(FP8X4), lhsT_scale=x_scale[:, j, :],
                     rhs=rew_codes[h][:].bitcast(FP8X4), rhs_scale=rew_scales[h][:], start=True, stop=True,
                 )
-                nc.scalar.activation(u[:, j, :], y[:], TANH, bias=bias[:, j : j + 1], scale=1.5)
+                ys.append(y)
+        util = []
+        for n, (h, c0, w) in enumerate(chunks):
+            u = sb.tile([P, PACK, w], F32, name=f"util{n}")
+            for j in range(PACK):
+                nc.scalar.activation(u[:, j, :], ys[PACK * h + j][:, c0 : c0 + w], TANH, bias=bias[:, j : j + 1], scale=1.5)
             util.append(u)
 
         pert_bf = sb.tile([P, R, PACK], BF16, name="pert_bf", align_bytes=64)
@@ -114,12 +113,10 @@ def tile_picked_yevos_tanh_p_kernel(
         pert_scales = sb.tile([P, R], U8, name="pert_scales", align_bytes=64)
         nc.vector.quantize_mx(pert_codes[:].bitcast(FP8X4), pert_scales[:], pert_bf[:].rearrange("p w j -> p (w j)"))
 
-        isig_wide = isig_sb[:, 0:span:RUN].unsqueeze(1).unsqueeze(3).to_broadcast([P, W // LINE, PACK, LINE])
-        wu = []
-        for h in range(HALVES):
-            wu_bf = sb.tile([P, W, PACK], BF16, name=f"wu_bf{h}", align_bytes=64)
-            nc.vector.tensor_tensor(words_by_line(wu_bf[:]), rows_by_line(util[h][:]), isig_wide, MULT)
-            wu.append(wu_bf)
+        wu = [sb.tile([P, W, PACK], BF16, name=f"wu_bf{h}", align_bytes=64) for h in range(HALVES)]
+        for n, (h, c0, w) in enumerate(chunks):
+            isig_wide = isig_sb[:].unsqueeze(1).unsqueeze(3).to_broadcast([P, w // LINE, PACK, LINE])
+            nc.vector.tensor_tensor(words_by_line(wu[h][:, c0 : c0 + w, :]), rows_by_line(util[n][:]), isig_wide, MULT)
 
         decayed = util[0][:, 0:HALVES, :]
         nc.scalar.mul(decayed, theta_raw[:].rearrange("p (h w) -> p h w", h=HALVES), 0.98)

from contextlib import ExitStack

import concourse.mybir as mybir

K, T, S, V, R = 512, 2048, 512, 256, 128
FLOPS = 2 * K * S * V + 2 * S * R * V

F32 = mybir.dt.float32
BF16 = mybir.dt.bfloat16
I32 = mybir.dt.int32
U32 = mybir.dt.uint32
U16 = mybir.dt.uint16
U8 = mybir.dt.uint8
FP8X4 = mybir.dt.float8_e4m3fn_x4
MULT = mybir.AluOpType.mult
ADD = mybir.AluOpType.add
TANH = mybir.ActivationFunctionType.Tanh

P = 128
PACK = 4
HALVES = 2
W = V // HALVES
LINE = 2
HEAD = 256


def rows_by_line(ap):
    return ap.rearrange("p j (c i) -> p c j i", i=LINE)


def words_by_line(ap):
    return ap.rearrange("p (c i) j -> p c j i", i=LINE)


def tile_picked_yevos_tanh_p_kernel(
    tc, x_words, x_scales, rew, pert, base, isig, theta, offs, out
):
    nc = tc.nc
    with ExitStack() as ctx:
        sb = ctx.enter_context(tc.tile_pool(name="sb", bufs=1))
        psum = ctx.enter_context(tc.psum_pool(name="psum", bufs=1))

        offsets = sb.tile([P, S // 16], U16, name="offsets")
        nc.sync.dma_start(offsets[:], offs)

        all_scales = sb.tile([P, T], U8, name="all_scales", align_bytes=64)
        nc.vector.memset(all_scales[:].bitcast(I32), 0)
        scale_rows = x_scales[0].rearrange("(q r) c -> r q c", r=4)

        rew_rows = rew.rearrange("(p j) v -> p j v", j=PACK)
        rew_raw = [sb.tile([P, PACK, W], F32, name=f"rew_raw{h}") for h in range(HALVES)]
        nc.sync.dma_start(rew_raw[0][:], rew_rows[:, :, 0:W])
        all_words = sb.tile([P, T], U32, name="all_words", align_bytes=64)
        word_rows = x_words[0].rearrange("p c b -> p (c b)").bitcast(I32)
        nc.sync.dma_start(all_words[:, 0:HEAD].bitcast(I32), word_rows[:, 0:HEAD])
        for r in range(4):
            nc.sync.dma_start(all_scales[r:P:32, :].bitcast(I32), scale_rows[r].bitcast(I32))
        nc.sync.dma_start(all_words[:, HEAD:T].bitcast(I32), word_rows[:, HEAD:T])
        nc.sync.dma_start(rew_raw[1][:], rew_rows[:, :, W:V])
        pert_raw = sb.tile([P, PACK, R], F32, name="pert_raw")
        nc.sync.dma_start(pert_raw[:], pert.rearrange("(p j) r -> p j r", j=PACK))
        base_sb = sb.tile([P, PACK], F32, name="base_sb")
        nc.sync.dma_start(base_sb[:], base.rearrange("(p j) o -> p (j o)", j=PACK))
        isig_sb = sb.tile([P, PACK], F32, name="isig_sb")
        nc.sync.dma_start(isig_sb[:], isig.rearrange("(p j) o -> p (j o)", j=PACK))
        theta_raw = sb.tile([P, V], F32, name="theta_raw")
        nc.sync.dma_start(theta_raw[:], theta)
        bias = sb.tile([P, PACK], F32, name="bias")
        nc.gpsimd.tensor_scalar(bias[:], base_sb[:], 1.5, 0.0, MULT, ADD)

        picked_scales = sb.tile([P, S], U8, name="picked_scales", align_bytes=64)
        nc.vector.tensor_copy(picked_scales[:], all_scales[:].indirect(offsets[:]))

        rew_codes, rew_scales = [], []

        def quantise_rew(h):
            grouped = sb.tile([P, W, PACK], BF16, name=f"rew_bf{h}", align_bytes=64)
            nc.scalar.copy(words_by_line(grouped[:]), rows_by_line(rew_raw[h][:]))
            codes = sb.tile([P, W], U32, name=f"rew_codes{h}", align_bytes=64)
            scales = sb.tile([P, W], U8, name=f"rew_scales{h}", align_bytes=64)
            nc.vector.quantize_mx(codes[:].bitcast(FP8X4), scales[:], grouped[:].rearrange("p w j -> p (w j)"))
            rew_codes.append(codes)
            rew_scales.append(scales)

        quantise_rew(0)
        x_scale = sb.tile([P, PACK, P], U8, name="x_scale", align_bytes=64)
        nc.vector.tensor_copy(x_scale[:], picked_scales[:].rearrange("p (m j) -> p j m", j=PACK))
        x_codes = sb.tile([P, PACK, P], U32, name="x_codes", align_bytes=64)
        nc.vector.tensor_copy(x_codes[:].rearrange("p j m -> p m j"), all_words[:].indirect(offsets[:]))

        quantise_rew(1)

        chunks = [(0, 0, W), (1, 0, W // 2), (1, W // 2, W // 2)]
        ys = []
        for h in range(HALVES):
            for j in range(PACK):
                y = psum.tile([P, W], F32, name=f"y{h}{j}", tag=f"bank{PACK * h + j}")
                nc.tensor.matmul_mx(
                    y[:], lhsT=x_codes[:, j, :].bitcast(FP8X4), lhsT_scale=x_scale[:, j, :],
                    rhs=rew_codes[h][:].bitcast(FP8X4), rhs_scale=rew_scales[h][:], start=True, stop=True,
                )
                ys.append(y)
        util = []
        for n, (h, c0, w) in enumerate(chunks):
            u = sb.tile([P, PACK, w], F32, name=f"util{n}")
            for j in range(PACK):
                nc.scalar.activation(u[:, j, :], ys[PACK * h + j][:, c0 : c0 + w], TANH, bias=bias[:, j : j + 1], scale=1.5)
            util.append(u)

        pert_bf = sb.tile([P, R, PACK], BF16, name="pert_bf", align_bytes=64)
        nc.vector.tensor_copy(words_by_line(pert_bf[:]), rows_by_line(pert_raw[:]))
        pert_codes = sb.tile([P, R], U32, name="pert_codes", align_bytes=64)
        pert_scales = sb.tile([P, R], U8, name="pert_scales", align_bytes=64)
        nc.vector.quantize_mx(pert_codes[:].bitcast(FP8X4), pert_scales[:], pert_bf[:].rearrange("p w j -> p (w j)"))

        wu = [sb.tile([P, W, PACK], BF16, name=f"wu_bf{h}", align_bytes=64) for h in range(HALVES)]
        for n, (h, c0, w) in enumerate(chunks):
            isig_wide = isig_sb[:].unsqueeze(1).unsqueeze(3).to_broadcast([P, w // LINE, PACK, LINE])
            nc.vector.tensor_tensor(words_by_line(wu[h][:, c0 : c0 + w, :]), rows_by_line(util[n][:]), isig_wide, MULT)

        decayed = util[0][:, 0:HALVES, :]
        nc.scalar.mul(decayed, theta_raw[:].rearrange("p (h w) -> p h w", h=HALVES), 0.98)

        grads = []
        for h in range(HALVES):
            codes = sb.tile([P, W], U32, name=f"wu_codes{h}", align_bytes=64)
            scales = sb.tile([P, W], U8, name=f"wu_scales{h}", align_bytes=64)
            nc.vector.quantize_mx(codes[:].bitcast(FP8X4), scales[:], wu[h][:].rearrange("p w j -> p (w j)"))
            grad = psum.tile([P, W], F32, name=f"grad{h}", tag=f"bank{h}")
            nc.tensor.matmul_mx(
                grad[:], lhsT=pert_codes[:].bitcast(FP8X4), lhsT_scale=pert_scales[:],
                rhs=codes[:].bitcast(FP8X4), rhs_scale=scales[:], start=True, stop=True,
            )
            grads.append(grad)
        for h in range(HALVES):
            res = sb.tile([P, W], F32, name=f"res{h}")
            nc.vector.scalar_tensor_tensor(res[:], grads[h][:], 0.5, decayed[:, h, :], MULT, ADD)
            nc.sync.dma_start(out[:, h * W : (h + 1) * W], res[:])
